import numpy as np
import ml_dtypes

BF16 = ml_dtypes.bfloat16


def bf(x):
    return np.asarray(x, np.float32).astype(BF16)


def f32(x):
    return np.asarray(x, np.float32)


def f64(x):
    return np.asarray(x).astype(np.float64)


def striped(idx):
    return np.tile(idx.reshape(-1, 16).T, (8, 1))


S, K, M, N, E, Q = 512, 512, 128, 256, 4, 64


def setup_inputs():
    return {"base": bf(np.random.standard_normal((M, S))), "x": bf(np.random.standard_normal((K, N))), "w": bf(np.random.standard_normal((E, K, M)) / np.sqrt(K)), "offs": striped(np.random.permutation(S)[:N])}


def reference(base, x, w, offs):
    idx = offs[:16].T.reshape(-1)
    z = f64(base).copy()
    for e in range(E):
        z[:, idx[e * Q : (e + 1) * Q]] += f64(w)[e].T @ f64(x)[:, e * Q : (e + 1) * Q]
    return z

@@ -1,0 +1,58 @@
+import concourse.mybir as mybir
+from concourse.masks import make_identity
+
+BF16, F32, U16 = mybir.dt.bfloat16, mybir.dt.float32, mybir.dt.uint16
+
+P = 128
+S = 512
+K = 512
+KB = K // P
+M = 128
+N = 256
+E = 4
+Q = N // E
+QC = Q // 16
+
+FLOPS = 2 * K * M * N
+
+
+def tile_scatter_matmul_kernel(tc, base, x, w, offs, out):
+    nc = tc.nc
+    with (
+        tc.tile_pool(name="held", bufs=1) as held,
+        tc.psum_pool(name="psum", bufs=1) as psum,
+    ):
+        offsets = held.tile([P, N // 16], U16, name="offsets")
+        nc.sync.dma_start(offsets[:], offs)
+        base_tile = held.tile([P, S], BF16, name="base_tile")
+        nc.sync.dma_start(base_tile[:], base)
+        x_tile = held.tile([P, KB, N], BF16, name="x_tile")
+        nc.scalar.dma_start(x_tile[:], x.rearrange("(kb p) n -> p kb n", p=P))
+        w_tiles = []
+        for e in range(E):
+            w_tile = held.tile([P, KB, M], BF16, name="w%d" % e)
+            queue = nc.sync if e % 2 == 0 else nc.scalar
+            queue.dma_start(w_tile[:], w[e].rearrange("(kb p) m -> p kb m", p=P))
+            w_tiles.append(w_tile)
+
+        ident = held.tile([P, P], BF16, name="ident")
+        make_identity(nc, ident[:])
+
+        window = psum.tile([P, S], F32, name="window")
+        nc.tensor.matmul(window[:], ident[:], base_tile[:], start=True, stop=False)
+
+        for e in range(E):
+            places = window[:].indirect(offsets[:, e * QC : (e + 1) * QC])
+            for kb in range(KB):
+                last = e == E - 1 and kb == KB - 1
+                nc.tensor.matmul(
+                    places,
+                    w_tiles[e][:, kb, :],
+                    x_tile[:, kb, e * Q : (e + 1) * Q],
+                    start=False,
+                    stop=last,
+                )
+
+        staged = held.tile([P, S], F32, name="staged")
+        nc.vector.tensor_copy(staged[:], window[:])
+        nc.sync.dma_start(out, staged[:])

@@ -27,12 +27,12 @@ def tile_scatter_matmul_kernel(tc, base, x, w, offs, out):
         base_tile = held.tile([P, S], BF16, name="base_tile")
         nc.sync.dma_start(base_tile[:], base)
         x_tile = held.tile([P, KB, N], BF16, name="x_tile")
-        nc.scalar.dma_start(x_tile[:], x.rearrange("(kb p) n -> p kb n", p=P))
+        nc.scalar.dma_start(x_tile[:], x.rearrange("(p kb) n -> p kb n", kb=KB))
         w_tiles = []
         for e in range(E):
             w_tile = held.tile([P, KB, M], BF16, name="w%d" % e)
             queue = nc.sync if e % 2 == 0 else nc.scalar
-            queue.dma_start(w_tile[:], w[e].rearrange("(kb p) m -> p kb m", p=P))
+            queue.dma_start(w_tile[:], w[e].rearrange("(p kb) m -> p kb m", kb=KB))
             w_tiles.append(w_tile)
 
         ident = held.tile([P, P], BF16, name="ident")

@@ -13,6 +13,8 @@ E = 4
 Q = N // E
 QC = Q // 16
 
+WARM = 6
+
 FLOPS = 2 * K * M * N
 
 
@@ -22,6 +24,12 @@ def tile_scatter_matmul_kernel(tc, base, x, w, offs, out):
         tc.tile_pool(name="held", bufs=1) as held,
         tc.psum_pool(name="psum", bufs=1) as psum,
     ):
+        warm_in = held.tile([P, S], BF16, name="warm_in")
+        nc.gpsimd.memset(warm_in[:], 0.0)
+        warm_out = psum.tile([P, S], F32, name="warm_out")
+        for i in range(WARM):
+            nc.tensor.matmul(warm_out[:], warm_in[:, 0:P], warm_in[:], start=True, stop=True)
+
         offsets = held.tile([P, N // 16], U16, name="offsets")
         nc.sync.dma_start(offsets[:], offs)
         base_tile = held.tile([P, S], BF16, name="base_tile")

@@ -13,7 +13,7 @@ E = 4
 Q = N // E
 QC = Q // 16
 
-WARM = 6
+WARM = 4
 
 FLOPS = 2 * K * M * N
 

@@ -30,17 +30,16 @@ def tile_scatter_matmul_kernel(tc, base, x, w, offs, out):
         for i in range(WARM):
             nc.tensor.matmul(warm_out[:], warm_in[:, 0:P], warm_in[:], start=True, stop=True)
 
-        offsets = held.tile([P, N // 16], U16, name="offsets")
-        nc.sync.dma_start(offsets[:], offs)
         base_tile = held.tile([P, S], BF16, name="base_tile")
         nc.sync.dma_start(base_tile[:], base)
+        offsets = held.tile([P, N // 16], U16, name="offsets")
+        nc.sync.dma_start(offsets[:], offs)
         x_tile = held.tile([P, KB, N], BF16, name="x_tile")
-        nc.scalar.dma_start(x_tile[:], x.rearrange("(p kb) n -> p kb n", kb=KB))
+        nc.sync.dma_start(x_tile[:], x.rearrange("(p kb) n -> p kb n", kb=KB))
         w_tiles = []
         for e in range(E):
             w_tile = held.tile([P, KB, M], BF16, name="w%d" % e)
-            queue = nc.sync if e % 2 == 0 else nc.scalar
-            queue.dma_start(w_tile[:], w[e].rearrange("(p kb) m -> p kb m", kb=KB))
+            nc.sync.dma_start(w_tile[:], w[e].rearrange("(p kb) m -> p kb m", kb=KB))
             w_tiles.append(w_tile)
 
         ident = held.tile([P, P], BF16, name="ident")

@@ -13,7 +13,7 @@ E = 4
 Q = N // E
 QC = Q // 16
 
-WARM = 4
+WARM = 2
 
 FLOPS = 2 * K * M * N
 

@@ -25,7 +25,7 @@ def tile_scatter_matmul_kernel(tc, base, x, w, offs, out):
         tc.psum_pool(name="psum", bufs=1) as psum,
     ):
         warm_in = held.tile([P, S], BF16, name="warm_in")
-        nc.gpsimd.memset(warm_in[:], 0.0)
+        nc.vector.memset(warm_in[:], 0.0)
         warm_out = psum.tile([P, S], F32, name="warm_out")
         for i in range(WARM):
             nc.tensor.matmul(warm_out[:], warm_in[:, 0:P], warm_in[:], start=True, stop=True)

@@ -14,6 +14,7 @@ Q = N // E
 QC = Q // 16
 
 WARM = 2
+ROW_ALIGN = 256
 
 FLOPS = 2 * K * M * N
 
@@ -30,15 +31,15 @@ def tile_scatter_matmul_kernel(tc, base, x, w, offs, out):
         for i in range(WARM):
             nc.tensor.matmul(warm_out[:], warm_in[:, 0:P], warm_in[:], start=True, stop=True)
 
-        base_tile = held.tile([P, S], BF16, name="base_tile")
+        base_tile = held.tile([P, S], BF16, name="base_tile", align_bytes=ROW_ALIGN)
         nc.sync.dma_start(base_tile[:], base)
         offsets = held.tile([P, N // 16], U16, name="offsets")
         nc.sync.dma_start(offsets[:], offs)
-        x_tile = held.tile([P, KB, N], BF16, name="x_tile")
+        x_tile = held.tile([P, KB, N], BF16, name="x_tile", align_bytes=ROW_ALIGN)
         nc.sync.dma_start(x_tile[:], x.rearrange("(p kb) n -> p kb n", kb=KB))
         w_tiles = []
         for e in range(E):
-            w_tile = held.tile([P, KB, M], BF16, name="w%d" % e)
+            w_tile = held.tile([P, KB, M], BF16, name="w%d" % e, align_bytes=ROW_ALIGN)
             nc.sync.dma_start(w_tile[:], w[e].rearrange("(p kb) m -> p kb m", kb=KB))
             w_tiles.append(w_tile)
 
@@ -60,6 +61,6 @@ def tile_scatter_matmul_kernel(tc, base, x, w, offs, out):
                     stop=last,
                 )
 
-        staged = held.tile([P, S], F32, name="staged")
+        staged = held.tile([P, S], F32, name="staged", align_bytes=ROW_ALIGN)
         nc.vector.tensor_copy(staged[:], window[:])
         nc.sync.dma_start(out, staged[:])

import concourse.mybir as mybir
from concourse.masks import make_identity

BF16, F32, U16 = mybir.dt.bfloat16, mybir.dt.float32, mybir.dt.uint16

P = 128
S = 512
K = 512
KB = K // P
M = 128
N = 256
E = 4
Q = N // E
QC = Q // 16

WARM = 2
ROW_ALIGN = 256

FLOPS = 2 * K * M * N


def tile_scatter_matmul_kernel(tc, base, x, w, offs, out):
    nc = tc.nc
    with (
        tc.tile_pool(name="held", bufs=1) as held,
        tc.psum_pool(name="psum", bufs=1) as psum,
    ):
        warm_in = held.tile([P, S], BF16, name="warm_in")
        nc.vector.memset(warm_in[:], 0.0)
        warm_out = psum.tile([P, S], F32, name="warm_out")
        for i in range(WARM):
            nc.tensor.matmul(warm_out[:], warm_in[:, 0:P], warm_in[:], start=True, stop=True)

        base_tile = held.tile([P, S], BF16, name="base_tile", align_bytes=ROW_ALIGN)
        nc.sync.dma_start(base_tile[:], base)
        offsets = held.tile([P, N // 16], U16, name="offsets")
        nc.sync.dma_start(offsets[:], offs)
        x_tile = held.tile([P, KB, N], BF16, name="x_tile", align_bytes=ROW_ALIGN)
        nc.sync.dma_start(x_tile[:], x.rearrange("(p kb) n -> p kb n", kb=KB))
        w_tiles = []
        for e in range(E):
            w_tile = held.tile([P, KB, M], BF16, name="w%d" % e, align_bytes=ROW_ALIGN)
            nc.sync.dma_start(w_tile[:], w[e].rearrange("(p kb) m -> p kb m", kb=KB))
            w_tiles.append(w_tile)

        ident = held.tile([P, P], BF16, name="ident")
        make_identity(nc, ident[:])

        window = psum.tile([P, S], F32, name="window")
        nc.tensor.matmul(window[:], ident[:], base_tile[:], start=True, stop=False)

        for e in range(E):
            places = window[:].indirect(offsets[:, e * QC : (e + 1) * QC])
            for kb in range(KB):
                last = e == E - 1 and kb == KB - 1
                nc.tensor.matmul(
                    places,
                    w_tiles[e][:, kb, :],
                    x_tile[:, kb, e * Q : (e + 1) * Q],
                    start=False,
                    stop=last,
                )

        staged = held.tile([P, S], F32, name="staged", align_bytes=ROW_ALIGN)
        nc.vector.tensor_copy(staged[:], window[:])
        nc.sync.dma_start(out, staged[:])
